import numpy as np
import ml_dtypes


def mxq(x, axis, fmt="e4m3"):
    dtype, down = {"e4m3": (ml_dtypes.float8_e4m3fn, 7), "e5m2": (ml_dtypes.float8_e5m2, 14)}[fmt]
    v = np.moveaxis(np.asarray(x, np.float32).astype(ml_dtypes.bfloat16).astype(np.float64), axis, -1)
    blocks = v.reshape(v.shape[:-1] + (-1, 32))
    amax = np.abs(blocks).max(-1, keepdims=True)
    byte = np.maximum(np.where(amax > 0, np.frexp(amax)[1] - 1 + 127, 0) - down, 1)
    scale = np.exp2(byte - 127.0)
    codes = (blocks / scale).astype(np.float32).astype(dtype).astype(np.float64)
    return np.moveaxis((codes * scale).reshape(v.shape), -1, axis)


WIDE = False


def mx_kscale(k):
    if not WIDE:
        return np.ones(k)
    levels = np.array([10, -10, 5, -5, 0])
    if k % 512:
        return np.exp2(np.random.permutation(np.resize(levels, k // 32))).repeat(32)
    a = np.empty((k // 512, 16))
    for p in range(k // 512):
        a[p, :8] = np.random.permutation(np.resize(levels, 8))
        for g in range(8):
            far = levels[np.abs(levels - a[p, g]) >= 10]
            a[p, g + 8] = far[np.random.randint(len(far))]
    return np.exp2(a.ravel()).repeat(32)


def f64(x):
    return np.asarray(x).astype(np.float64)


def striped(idx):
    return np.tile(idx.reshape(-1, 16).T, (8, 1)).astype(np.uint16)


def unstriped(offs):
    return offs[:16].T.reshape(-1).astype(np.int64)


E2M1 = np.array([0.0, 0.5, 1.0, 1.5, 2.0, 3.0, 4.0, 6.0, -0.0, -0.5, -1.0, -1.5, -2.0, -3.0, -4.0, -6.0])


def pack_weight(w, fmt):
    k, n = w.shape
    w = f64(np.asarray(w, np.float32).astype(ml_dtypes.bfloat16)).reshape(k // 32, 32, n)
    amax = np.abs(w).max(1)
    if fmt == "e4m3":
        byte = np.frexp(amax)[1] - 1 + 127 - 7
    else:
        mant, ex = np.frexp(amax / 6.0)
        byte = np.where(mant > 0.5, ex, ex - 1) + 127
    byte = np.clip(np.where(amax > 0, byte, 1), 1, 254)
    scaled = (w * np.exp2(127.0 - byte)[:, None, :]).reshape(k, n).astype(np.float32)
    by_word = np.ascontiguousarray(scaled.reshape(k // 512, 128, 4, n).transpose(0, 1, 3, 2))
    if fmt == "e4m3":
        words = by_word.astype(ml_dtypes.float8_e4m3fn).view(np.uint8)
    else:
        c = by_word.astype(ml_dtypes.float4_e2m1fn).view(np.uint8) & 0xF
        words = (c[..., 0::2] | (c[..., 1::2] << 4)).reshape(k // 512, 128, 2 * n)
    return np.ascontiguousarray(words), np.ascontiguousarray(byte.astype(np.uint8).reshape(k // 512, 16, n))


def unpack_weight(words, scales, fmt):
    g, _, n = scales.shape
    words = np.ascontiguousarray(words).reshape(g, 128, n, -1)
    if fmt == "e4m3":
        vals = words.view(ml_dtypes.float8_e4m3fn).astype(np.float64)
    else:
        nib = np.empty((g, 128, n, 4), np.uint8)
        nib[..., 0::2] = words & 0xF
        nib[..., 1::2] = words >> 4
        vals = E2M1[nib]
    vals = vals * np.repeat(np.exp2(scales.astype(np.float64) - 127.0), 8, axis=1)[..., None]
    return vals.transpose(0, 1, 3, 2).reshape(g * 512, n)


def gelu(v):
    return 0.5 * v * (1.0 + np.tanh(np.sqrt(2.0 / np.pi) * (v + 0.044715 * v**3)))


K, T, S, P, H, T2, N, R = 1536, 4096, 1024, 1024, 1024, 2048, 512, 128

def setup_inputs():
    n = np.random.standard_normal
    s = mx_kscale(K)[:, None]
    u = mx_kscale(H)[:, None]
    d = {}
    d["tab_words"], d["tab_scales"] = pack_weight(n((K, T)) * s, "e4m3")
    d["offs"] = striped(np.random.permutation(T)[:S])
    d["w1"] = (1.5 * n((K, H)) / K ** 0.5 / s).astype(np.float32)
    d["gm"] = (1.5 * n((H, S)) * u).astype(np.float32)
    d["page0"] = (n((H, T2)) * u).astype(np.float32)
    d["wgs"] = np.exp(0.3 * n((R, S))).astype(np.float32)
    d["offs2"] = striped(np.random.permutation(T2)[:S])
    d["offs3"] = striped(np.random.permutation(T2)[:P])
    d["gain"] = np.exp(0.3 * n(H)).astype(np.float32)
    d["w2"] = (0.48 * n((H, N)) / H ** 0.5 / u).astype(np.float32)
    d["w4_words"], d["w4_scales"] = pack_weight(0.35 * n((H, N)) / H ** 0.5 / u, "e2m1")
    d["bias"] = (0.3 * n(N)).astype(np.float32)
    d["page1"] = (0.4 * n((N, T2))).astype(np.float32)
    d["wgo"] = np.exp(0.3 * n((R, P))).astype(np.float32)
    d["offs4"] = striped(np.random.permutation(T2)[:P])
    return d

def reference(tab_words, tab_scales, offs, w1, gm, page0, wgs, offs2, offs3, gain, w2, w4_words, w4_scales, bias, page1, wgo, offs4):
    v = unpack_weight(tab_words, tab_scales, "e4m3")[:, unstriped(offs)]
    hum = mxq(f64(w1), 0, "e4m3").T @ v
    h = f64(gm) / (1.0 + np.abs(hum))
    page = f64(page0).copy()
    page[:, unstriped(offs2)] = np.tile(f64(wgs), (H // R, 1)) * h
    x = page[:, unstriped(offs3)] * f64(gain)[:, None]
    xq = mxq(x, 0, "e4m3")
    wave = np.sin(mxq(f64(w2), 0, "e4m3").T @ xq)
    drift = unpack_weight(w4_words, w4_scales, "e2m1").T @ xq
    y = wave + drift + f64(bias)[:, None]
    out = f64(page1).copy()
    out[:, unstriped(offs4)] = np.tile(f64(wgo), (N // R, 1)) * y
    return out

@@ -1,0 +1,369 @@
+from contextlib import ExitStack
+
+import concourse.mybir as mybir
+from concourse.masks import make_identity
+
+K, T, S, H, T2, N = 1536, 4096, 1024, 1024, 2048, 512
+FLOPS = 2 * K * H * S + 2 * 2 * H * N * S
+
+F32 = mybir.dt.float32
+BF16 = mybir.dt.bfloat16
+I32 = mybir.dt.int32
+U32 = mybir.dt.uint32
+U16 = mybir.dt.uint16
+U8 = mybir.dt.uint8
+FP8X4 = mybir.dt.float8_e4m3fn_x4
+FP4X4 = mybir.dt.float4_e2m1fn_x4
+ACT = mybir.ActivationFunctionType
+MULT = mybir.AluOpType.mult
+
+P = 128
+KB = 1024
+HALF = 512
+QUARTER = 256
+
+TAB, PAGE_HI, PICK_LO, XQ = 0, 0, 32, 32
+PAGE_LO, STAGE2, YS = 48, 48, 64
+RAW = 80
+GATHERED, TAB_SCALES, WGS = 112, 125, 129
+ROUNDED = 133
+W1Q, W2Q, W4 = 141, 156, 161
+SMALL = 164
+NEG_LN_W = 165
+LOGS = 181
+DAMP = 189
+GM = 205
+PLANES_LO = 229
+
+
+def tile_list_dryer_airflow_page_kernel(
+    tc, tab_words, tab_scales, offs, w1, gm, page0, wgs, offs2, offs3, gain,
+    w2, w4_words, w4_scales, bias, page1, wgo, offs4, out,
+):
+    nc = tc.nc
+    with ExitStack() as ctx:
+        lists = ctx.enter_context(tc.tile_pool(name="lists", bufs=1))
+        sbuf = ctx.enter_context(tc.tile_pool(name="sbuf", bufs=1))
+        psum = ctx.enter_context(tc.psum_pool(name="psum", bufs=4))
+
+        def at(name, kb, shape, dtype):
+            return sbuf.tile(shape, dtype, name=name, offset=int(kb * KB), align_bytes=64)
+
+        def load_list(name, src):
+            tile = lists.tile([P, S // 16], U16, name=name)
+            nc.sync.dma_start(tile[:], src)
+            return tile
+
+        def entries(tile, first, count):
+            return tile[:, first // 16 : (first + count) // 16]
+
+        def load_weight(name, slot, rows):
+            raw = at(name, RAW + 8 * slot, [P, 4, HALF], F32)
+            nc.sync.dma_start(out=raw[:], in_=rows.rearrange("(p j) c -> p j c", j=4))
+            return raw
+
+        def interleave(copy, name, kb, planes, width):
+            woven = at(name, kb, [P, width, 4], BF16)
+            copy(
+                out=woven[:].rearrange("p (c i) j -> p c j i", i=4),
+                in_=planes.rearrange("p j (c i) -> p c j i", i=4),
+            )
+            return woven
+
+        def quantize(woven, codes, scales):
+            nc.vector.quantize_mx(
+                out=codes.bitcast(FP8X4), scales=scales, in_=woven[:].rearrange("p c j -> p (c j)")
+            )
+
+        def dealt(matrix, b):
+            return matrix[b * HALF : (b + 1) * HALF, :].rearrange("(p t) c -> p t c", t=4)
+
+        def load_page(name, kb, rows):
+            tile = at(name, kb, [P, T2], F32)
+            nc.sync.dma_start(out=tile[:], in_=rows)
+            return tile
+
+        ident = at("ident", SMALL, [P, P], F32)
+        make_identity(nc, ident[:])
+        tab_sc = at("tab_sc", TAB_SCALES, [P, T], U8)
+        nc.vector.memset(tab_sc[:].bitcast(I32), 0)
+        w4_sc = at("w4_sc", W4 + 2, [P, 2, N], U8)
+        nc.gpsimd.memset(w4_sc[:].rearrange("p a c -> p (a c)").bitcast(I32), 0)
+
+        w1_raw = {}
+        w1_raw[0, 0] = load_weight("w1_raw00", 0, w1[0:512, 0:HALF])
+        idx = load_list("idx", offs)
+        idx2 = load_list("idx2", offs2)
+        idx3 = load_list("idx3", offs3)
+        idx4 = load_list("idx4", offs4)
+        gain_sb = at("gain_sb", SMALL + 0.5, [P, 2, 4], F32)
+        nc.sync.dma_start(out=gain_sb[:], in_=gain.rearrange("(b p t) -> p b t", b=2, t=4))
+        wgs_sb = at("wgs_sb", WGS, [P, S], F32)
+        nc.sync.dma_start(out=wgs_sb[:], in_=wgs)
+        w1_raw[0, 1] = load_weight("w1_raw01", 1, w1[512:1024, 0:HALF])
+        for q in range(4):
+            nc.sync.dma_start(
+                out=tab_sc[32 * q : 32 * q + 12, :].bitcast(I32),
+                in_=tab_scales[:, 4 * q : 4 * q + 4, :].bitcast(I32),
+            )
+        w1_raw[0, 2] = load_weight("w1_raw02", 2, w1[1024:1536, 0:HALF])
+        tab = []
+        for a in range(3):
+            words = at("tab%d" % a, TAB + 16 * a, [P, T], I32)
+            nc.sync.dma_start(out=words[:], in_=tab_words[a].rearrange("p n t -> p (n t)").bitcast(I32))
+            tab.append(words)
+
+        w1_q = {}
+        w1_s = {}
+
+        def prepare_w1(copy, b, a):
+            n = 3 * b + a
+            woven = interleave(copy, "w1_bf%d" % n, ROUNDED + 4 * (n % 2), w1_raw[b, a][:], HALF)
+            w1_q[b, a] = at("w1_q%d" % n, W1Q + 2 * n, [P, HALF], U32)
+            w1_s[b, a] = at("w1_s%d" % n, W1Q + 12 + n / 2, [P, HALF], U8)
+            quantize(woven, w1_q[b, a][:], w1_s[b, a][:])
+
+        for a in range(3):
+            prepare_w1(nc.vector.tensor_copy, 0, a)
+
+        ln_w = at("ln_w", DAMP + 8, [P, 32, 32], F32)
+        for half in range(2):
+            bank = psum.tile([P, 4, P], F32, name="bank", tag="sum")
+            for i in range(4):
+                jb = 4 * half + i
+                nc.tensor.transpose(bank[:, i, :], wgs_sb[:, jb * P : (jb + 1) * P], ident[:])
+            nc.scalar.activation(
+                out=ln_w[:, 16 * half : 16 * half + 16, :].rearrange("p (i t) m -> p i t m", t=4),
+                in_=bank[:].rearrange("p i (m t) -> p i t m", t=4),
+                func=ACT.Ln,
+            )
+        neg_ln_w = at("neg_ln_w", NEG_LN_W, [P, 32, P], F32)
+        for q in range(4):
+            nc.scalar.activation(
+                out=neg_ln_w[:, :, 32 * q : 32 * q + 32], in_=ln_w[:], func=ACT.Copy, scale=-1.0
+            )
+
+        v_s = at("v_s", GATHERED + 12, [P, S], U8)
+        nc.vector.tensor_copy(v_s[:], tab_sc[:].indirect(idx[:]))
+        v_q = []
+        for a in range(3):
+            picked = at("v_q%d" % a, GATHERED + 4 * a, [P, S], U32)
+            width = HALF if a == 2 else S
+            for j0 in range(0, S, width):
+                nc.vector.tensor_copy(
+                    picked[:, j0 : j0 + width],
+                    tab[a][:].bitcast(U32).indirect(entries(idx, j0, width)),
+                )
+            v_q.append(picked)
+
+        pages = {}
+        gm_sb = {}
+        gm_sb[0, 0] = at("gm00", GM, [P, 4, HALF], F32)
+        for t in range(4):
+            pages[0, t] = load_page("page0%d" % t, PAGE_LO + 8 * t, dealt(page0, 0)[:, t, :])
+            nc.sync.dma_start(out=gm_sb[0, 0][:, t, :], in_=dealt(gm, 0)[:, t, 0:HALF])
+            if t == 0:
+                w1_raw[1, 0] = load_weight("w1_raw10", 3, w1[0:512, HALF:H])
+                w1_raw[1, 1] = load_weight("w1_raw11", 0, w1[512:1024, HALF:H])
+
+        for a in range(2):
+            prepare_w1(nc.vector.tensor_copy, 1, a)
+
+        def load_gm(b, jh):
+            n = 2 * b + jh
+            gm_sb[b, jh] = at("gm%d%d" % (b, jh), GM + 8 * (n % 3), [P, 4, HALF], F32)
+            nc.sync.dma_start(out=gm_sb[b, jh][:], in_=dealt(gm, b)[:, :, jh * HALF : (jh + 1) * HALF])
+
+        load_gm(0, 1)
+        w1_raw[1, 2] = load_weight("w1_raw12", 1, w1[1024:1536, HALF:H])
+        for t in range(4):
+            pages[1, t] = load_page("page1%d" % t, PAGE_HI + 8 * t, dealt(page0, 1)[:, t, :])
+            if t == 0:
+                load_gm(1, 0)
+        w2_raw = [load_weight("w2_raw%d" % b, 2 + b, w2[b * HALF : (b + 1) * HALF, :]) for b in range(2)]
+        w4_q = at("w4_q", W4, [P, 2, 2 * N], U8)
+        nc.sync.dma_start(
+            out=w4_q[:].bitcast(I32), in_=w4_words.rearrange("a p c -> p a c").bitcast(I32)
+        )
+        for q in range(4):
+            nc.sync.dma_start(
+                out=w4_sc[32 * q : 32 * q + 4, :, :].bitcast(I32),
+                in_=w4_scales[:, 4 * q : 4 * q + 4, :].rearrange("a r c -> r a c").bitcast(I32),
+            )
+        wgo_sb = at("wgo_sb", TAB_SCALES, [P, S], F32)
+        nc.sync.dma_start(out=wgo_sb[:], in_=wgo)
+        bias_sb = at("bias_sb", SMALL + 0.5625, [P, 4], F32)
+        with nc.allow_non_contiguous_dma(reason="one bias value a partition"):
+            nc.sync.dma_start(out=bias_sb[:], in_=bias.rearrange("(nb p) -> p nb", p=P))
+
+        pick_lo = [at("pick_lo%d" % t, PICK_LO + 4 * t, [P, S], F32) for t in range(4)]
+        pick_first = at("pick_first", WGS, [P, 4, QUARTER], F32)
+        damp = {}
+
+        def stage_one(b, jh):
+            logs = at("logs%d%d" % (b, jh), LOGS, [P, 4, HALF], F32)
+            for i in range(4):
+                cols = slice(jh * HALF + i * P, jh * HALF + (i + 1) * P)
+                hum = psum.tile([P, HALF], F32, name="hum", tag="acc")
+                for a in range(3):
+                    nc.tensor.matmul_mx(
+                        out=hum[:],
+                        lhsT=v_q[a][:, cols].bitcast(FP8X4),
+                        lhsT_scale=v_s[4 * a : P, cols],
+                        rhs=w1_q[b, a][:].bitcast(FP8X4),
+                        rhs_scale=w1_s[b, a][:],
+                        start=(a == 0),
+                        stop=(a == 2),
+                    )
+                nc.scalar.activation(
+                    out=logs[:, i, :].rearrange("p (t m) -> p t m", t=4),
+                    in_=hum[:].rearrange("p (m t) -> p t m", t=4),
+                    func=ACT.Abs,
+                )
+                nc.scalar.activation(out=logs[:, i, :], in_=logs[:, i, :], func=ACT.Ln, bias=1.0)
+            damp[b, jh] = at("damp%d%d" % (b, jh), DAMP + 8 * jh, [P, 4, HALF], F32)
+            for t in range(4):
+                total = psum.tile([P, 4, P], F32, name="total", tag="sum")
+                for i in range(4):
+                    nc.tensor.matmul(
+                        total[:, i, :], lhsT=neg_ln_w[:, 16 * jh + 4 * i + t, :], rhs=ident[:],
+                        is_transpose=True, start=(i == 0), stop=False,
+                    )
+                for i in range(4):
+                    nc.tensor.matmul(
+                        total[:, i, :], lhsT=logs[:, i, t * P : (t + 1) * P], rhs=ident[:],
+                        is_transpose=True, start=False, stop=(i == 3),
+                    )
+                nc.scalar.activation(
+                    out=damp[b, jh][:, t, :], in_=total[:].rearrange("p i j -> p (i j)"),
+                    func=ACT.Exp, scale=-1.0,
+                )
+                nc.vector.tensor_tensor(
+                    pages[b, t][:].indirect(entries(idx2, jh * HALF, HALF)),
+                    damp[b, jh][:, t, :], gm_sb[b, jh][:, t, :], MULT,
+                )
+                if (b, jh, t) == (0, 1, 0):
+                    prepare_w1(nc.scalar.copy, 1, 2)
+                if jh == 1 and b == 0:
+                    nc.vector.tensor_copy(pick_lo[t][:], pages[b, t][:].indirect(idx3[:]))
+                if jh == 1 and b == 1:
+                    nc.vector.tensor_copy(
+                        pick_first[:, t, :], pages[b, t][:].indirect(entries(idx3, 0, QUARTER))
+                    )
+
+        stage_one(0, 0)
+        load_gm(1, 1)
+        stage_one(0, 1)
+        airflow = [load_page("air%d" % nb, RAW + 8 * nb, page1[nb * P : (nb + 1) * P, :]) for nb in range(2)]
+        stage_one(1, 0)
+        stage_one(1, 1)
+
+        table_warm = at("table_warm", SMALL + 0.625, [P, 1], F32)
+        nc.scalar.activation(out=table_warm[:], in_=damp[1, 1][:, 3, 0:1], func=ACT.Sin, scale=0.0)
+
+        w2_q = at("w2_q", W2Q, [P, 2, N], U32)
+        w2_s = at("w2_s", W2Q + 4, [P, 2, N], U8)
+        for b in range(2):
+            woven = interleave(nc.scalar.copy, "w2_bf%d" % b, ROUNDED + 4 * b, w2_raw[b][:], N)
+            quantize(woven, w2_q[:, b, :], w2_s[:, b, :])
+        for nb in range(2, 4):
+            airflow.append(load_page("air%d" % nb, RAW + 8 * nb, page1[nb * P : (nb + 1) * P, :]))
+
+        planes = [at("planes0", PLANES_LO, [P, 4, S], BF16), at("planes1", PLANES_LO, [P, 4, S], BF16)]
+
+        def scale_plane(b, t, m0, width, picked):
+            nc.scalar.activation(
+                out=planes[b][:, t, m0 : m0 + width], in_=picked, func=ACT.Copy,
+                scale=gain_sb[:, b, t : t + 1],
+            )
+
+        for t in range(4):
+            scale_plane(0, t, 0, S, pick_lo[t][:])
+        x_q = [at("x_q%d" % b, XQ + 4 * b, [P, S], U32) for b in range(2)]
+        x_s = [at("x_s%d" % b, XQ + 8 + b, [P, S], U8) for b in range(2)]
+
+        def quantize_x(b, m0, width, kb):
+            cols = slice(m0, m0 + width)
+            woven = interleave(nc.scalar.copy, "x_bf%d_%d" % (b, m0), kb, planes[b][:, :, cols], width)
+            quantize(woven, x_q[b][:, cols], x_s[b][:, cols])
+
+        for mh in range(2):
+            quantize_x(0, mh * HALF, HALF, GM + 8 + 4 * mh)
+        for t in range(4):
+            scale_plane(1, t, 0, QUARTER, pick_first[:, t, :])
+        quantize_x(1, 0, QUARTER, NEG_LN_W + 3)
+        pick_second = at("pick_second", NEG_LN_W, [P, 4, QUARTER], F32)
+        pick_rest = at("pick_rest", NEG_LN_W + 4, [P, 4, HALF], F32)
+        for picked, m0, width in ((pick_second, QUARTER, QUARTER), (pick_rest, HALF, HALF)):
+            for t in range(4):
+                nc.vector.tensor_copy(
+                    picked[:, t, :], pages[1, t][:].indirect(entries(idx3, m0, width))
+                )
+
+        parts = {}
+
+        def products(mq):
+            wave = at("wave%d" % mq, STAGE2 + 8 * (mq % 2), [P, 2, N], F32)
+            drift = at("drift%d" % mq, STAGE2 + 8 * (mq % 2) + 4, [P, 2, N], F32)
+            for i in range(2):
+                cols = slice(mq * QUARTER + i * P, mq * QUARTER + (i + 1) * P)
+                phase = psum.tile([P, N], F32, name="phase", tag="acc")
+                line = psum.tile([P, N], F32, name="line", tag="acc")
+                for b in range(2):
+                    nc.tensor.matmul_mx(
+                        out=phase[:], lhsT=x_q[b][:, cols].bitcast(FP8X4), lhsT_scale=x_s[b][:, cols],
+                        rhs=w2_q[:, b, :].bitcast(FP8X4), rhs_scale=w2_s[:, b, :],
+                        start=(b == 0), stop=(b == 1),
+                    )
+                for b in range(2):
+                    nc.tensor.matmul_mx(
+                        out=line[:], lhsT=x_q[b][:, cols].bitcast(FP8X4), lhsT_scale=x_s[b][:, cols],
+                        rhs=w4_q[:, b, :].bitcast(FP4X4), rhs_scale=w4_sc[:, b, :],
+                        start=(b == 0), stop=(b == 1),
+                    )
+                nc.scalar.activation(out=wave[:, i, :], in_=phase[:], func=ACT.Sin)
+                nc.scalar.copy(out=drift[:, i, :], in_=line[:])
+            parts[mq] = (drift, wave)
+
+        def place(mq, nb):
+            total = psum.tile([P, 2, P], F32, name="total", tag="sum")
+            for k, part in enumerate(parts[mq]):
+                for i in range(2):
+                    nc.tensor.matmul(
+                        total[:, i, :], lhsT=part[:, i, nb * P : (nb + 1) * P], rhs=ident[:],
+                        is_transpose=True, start=(k == 0 and i == 0), stop=(k == 1 and i == 1),
+                    )
+            y = at("y%d%d" % (mq, nb), YS + 4 * mq + nb, [P, QUARTER], F32)
+            nc.scalar.activation(
+                out=y[:], in_=total[:].rearrange("p i m -> p (i m)"), func=ACT.Identity,
+                bias=bias_sb[:, nb : nb + 1],
+            )
+            nc.vector.tensor_tensor(
+                airflow[nb][:].indirect(entries(idx4, mq * QUARTER, QUARTER)),
+                y[:], wgo_sb[:, mq * QUARTER : (mq + 1) * QUARTER], MULT,
+            )
+            if mq == 3:
+                nc.sync.dma_start(out=out[nb * P : (nb + 1) * P, :], in_=airflow[nb][:])
+
+        products(0)
+        for t in range(4):
+            scale_plane(1, t, QUARTER, QUARTER, pick_second[:, t, :])
+        quantize_x(1, QUARTER, QUARTER, ROUNDED)
+        place(0, 0)
+        place(0, 1)
+        for t in range(4):
+            scale_plane(1, t, HALF, HALF, pick_rest[:, t, :])
+        quantize_x(1, HALF, HALF, ROUNDED + 4)
+        place(0, 2)
+        place(0, 3)
+        products(1)
+        for nb in range(4):
+            place(1, nb)
+        products(2)
+        place(2, 0)
+        place(2, 1)
+        products(3)
+        for nb in range(4):
+            place(3, nb)
+            if nb < 2:
+                place(2, nb + 2)

@@ -33,7 +33,7 @@ NEG_LN_W = 165
 LOGS = 181
 DAMP = 189
 GM = 205
-PLANES_LO = 229
+BANKS = ("even", "odd")
 
 
 def tile_list_dryer_airflow_page_kernel(
@@ -128,7 +128,7 @@ def tile_list_dryer_airflow_page_kernel(
 
         ln_w = at("ln_w", DAMP + 8, [P, 32, 32], F32)
         for half in range(2):
-            bank = psum.tile([P, 4, P], F32, name="bank", tag="sum")
+            bank = psum.tile([P, 4, P], F32, name="bank", tag=BANKS[1])
             for i in range(4):
                 jb = 4 * half + i
                 nc.tensor.transpose(bank[:, i, :], wgs_sb[:, jb * P : (jb + 1) * P], ident[:])
@@ -156,18 +156,15 @@ def tile_list_dryer_airflow_page_kernel(
                 )
             v_q.append(picked)
 
+        for a in range(3):
+            w1_raw[1, a] = load_weight("w1_raw1%d" % a, (3 + a) % 4, w1[512 * a : 512 * (a + 1), HALF:H])
+            prepare_w1(nc.vector.tensor_copy, 1, a)
         pages = {}
         gm_sb = {}
         gm_sb[0, 0] = at("gm00", GM, [P, 4, HALF], F32)
         for t in range(4):
             pages[0, t] = load_page("page0%d" % t, PAGE_LO + 8 * t, dealt(page0, 0)[:, t, :])
             nc.sync.dma_start(out=gm_sb[0, 0][:, t, :], in_=dealt(gm, 0)[:, t, 0:HALF])
-            if t == 0:
-                w1_raw[1, 0] = load_weight("w1_raw10", 3, w1[0:512, HALF:H])
-                w1_raw[1, 1] = load_weight("w1_raw11", 0, w1[512:1024, HALF:H])
-
-        for a in range(2):
-            prepare_w1(nc.vector.tensor_copy, 1, a)
 
         def load_gm(b, jh):
             n = 2 * b + jh
@@ -175,7 +172,6 @@ def tile_list_dryer_airflow_page_kernel(
             nc.sync.dma_start(out=gm_sb[b, jh][:], in_=dealt(gm, b)[:, :, jh * HALF : (jh + 1) * HALF])
 
         load_gm(0, 1)
-        w1_raw[1, 2] = load_weight("w1_raw12", 1, w1[1024:1536, HALF:H])
         for t in range(4):
             pages[1, t] = load_page("page1%d" % t, PAGE_HI + 8 * t, dealt(page0, 1)[:, t, :])
             if t == 0:
@@ -204,7 +200,7 @@ def tile_list_dryer_airflow_page_kernel(
             logs = at("logs%d%d" % (b, jh), LOGS, [P, 4, HALF], F32)
             for i in range(4):
                 cols = slice(jh * HALF + i * P, jh * HALF + (i + 1) * P)
-                hum = psum.tile([P, HALF], F32, name="hum", tag="acc")
+                hum = psum.tile([P, HALF], F32, name="hum", tag=BANKS[jh])
                 for a in range(3):
                     nc.tensor.matmul_mx(
                         out=hum[:],
@@ -223,7 +219,7 @@ def tile_list_dryer_airflow_page_kernel(
                 nc.scalar.activation(out=logs[:, i, :], in_=logs[:, i, :], func=ACT.Ln, bias=1.0)
             damp[b, jh] = at("damp%d%d" % (b, jh), DAMP + 8 * jh, [P, 4, HALF], F32)
             for t in range(4):
-                total = psum.tile([P, 4, P], F32, name="total", tag="sum")
+                total = psum.tile([P, 4, P], F32, name="total", tag=BANKS[1 - jh])
                 for i in range(4):
                     nc.tensor.matmul(
                         total[:, i, :], lhsT=neg_ln_w[:, 16 * jh + 4 * i + t, :], rhs=ident[:],
@@ -242,8 +238,6 @@ def tile_list_dryer_airflow_page_kernel(
                     pages[b, t][:].indirect(entries(idx2, jh * HALF, HALF)),
                     damp[b, jh][:, t, :], gm_sb[b, jh][:, t, :], MULT,
                 )
-                if (b, jh, t) == (0, 1, 0):
-                    prepare_w1(nc.scalar.copy, 1, 2)
                 if jh == 1 and b == 0:
                     nc.vector.tensor_copy(pick_lo[t][:], pages[b, t][:].indirect(idx3[:]))
                 if jh == 1 and b == 1:
@@ -269,7 +263,7 @@ def tile_list_dryer_airflow_page_kernel(
         for nb in range(2, 4):
             airflow.append(load_page("air%d" % nb, RAW + 8 * nb, page1[nb * P : (nb + 1) * P, :]))
 
-        planes = [at("planes0", PLANES_LO, [P, 4, S], BF16), at("planes1", PLANES_LO, [P, 4, S], BF16)]
+        planes = [at("planes0", LOGS, [P, 4, S], BF16), at("planes1", LOGS, [P, 4, S], BF16)]
 
         def scale_plane(b, t, m0, width, picked):
             nc.scalar.activation(
@@ -307,8 +301,8 @@ def tile_list_dryer_airflow_page_kernel(
             drift = at("drift%d" % mq, STAGE2 + 8 * (mq % 2) + 4, [P, 2, N], F32)
             for i in range(2):
                 cols = slice(mq * QUARTER + i * P, mq * QUARTER + (i + 1) * P)
-                phase = psum.tile([P, N], F32, name="phase", tag="acc")
-                line = psum.tile([P, N], F32, name="line", tag="acc")
+                phase = psum.tile([P, N], F32, name="phase", tag=BANKS[1])
+                line = psum.tile([P, N], F32, name="line", tag=BANKS[1])
                 for b in range(2):
                     nc.tensor.matmul_mx(
                         out=phase[:], lhsT=x_q[b][:, cols].bitcast(FP8X4), lhsT_scale=x_s[b][:, cols],
@@ -326,7 +320,7 @@ def tile_list_dryer_airflow_page_kernel(
             parts[mq] = (drift, wave)
 
         def place(mq, nb):
-            total = psum.tile([P, 2, P], F32, name="total", tag="sum")
+            total = psum.tile([P, 2, P], F32, name="total", tag=BANKS[0])
             for k, part in enumerate(parts[mq]):
                 for i in range(2):
                     nc.tensor.matmul(
@@ -348,11 +342,11 @@ def tile_list_dryer_airflow_page_kernel(
         products(0)
         for t in range(4):
             scale_plane(1, t, QUARTER, QUARTER, pick_second[:, t, :])
-        quantize_x(1, QUARTER, QUARTER, ROUNDED)
         place(0, 0)
-        place(0, 1)
+        quantize_x(1, QUARTER, QUARTER, ROUNDED)
         for t in range(4):
             scale_plane(1, t, HALF, HALF, pick_rest[:, t, :])
+        place(0, 1)
         quantize_x(1, HALF, HALF, ROUNDED + 4)
         place(0, 2)
         place(0, 3)

@@ -34,6 +34,7 @@ LOGS = 181
 DAMP = 189
 GM = 205
 BANKS = ("even", "odd")
+PRODUCT_BANKS = (1, 0, 1, 1)
 
 
 def tile_list_dryer_airflow_page_kernel(
@@ -263,31 +264,30 @@ def tile_list_dryer_airflow_page_kernel(
         for nb in range(2, 4):
             airflow.append(load_page("air%d" % nb, RAW + 8 * nb, page1[nb * P : (nb + 1) * P, :]))
 
-        planes = [at("planes0", LOGS, [P, 4, S], BF16), at("planes1", LOGS, [P, 4, S], BF16)]
-
-        def scale_plane(b, t, m0, width, picked):
+        def scale_plane(b, t, planes, picked):
             nc.scalar.activation(
-                out=planes[b][:, t, m0 : m0 + width], in_=picked, func=ACT.Copy,
-                scale=gain_sb[:, b, t : t + 1],
+                out=planes[:, t, :], in_=picked, func=ACT.Copy, scale=gain_sb[:, b, t : t + 1]
             )
 
+        planes_lo = at("planes_lo", LOGS, [P, 4, S], BF16)
         for t in range(4):
-            scale_plane(0, t, 0, S, pick_lo[t][:])
+            scale_plane(0, t, planes_lo, pick_lo[t][:])
         x_q = [at("x_q%d" % b, XQ + 4 * b, [P, S], U32) for b in range(2)]
         x_s = [at("x_s%d" % b, XQ + 8 + b, [P, S], U8) for b in range(2)]
 
-        def quantize_x(b, m0, width, kb):
+        def quantize_x(b, m0, width, kb, planes):
             cols = slice(m0, m0 + width)
-            woven = interleave(nc.scalar.copy, "x_bf%d_%d" % (b, m0), kb, planes[b][:, :, cols], width)
+            woven = interleave(nc.scalar.copy, "x_bf%d_%d" % (b, m0), kb, planes, width)
             quantize(woven, x_q[b][:, cols], x_s[b][:, cols])
 
         for mh in range(2):
-            quantize_x(0, mh * HALF, HALF, GM + 8 + 4 * mh)
+            quantize_x(0, mh * HALF, HALF, GM + 8 + 4 * mh, planes_lo[:, :, mh * HALF : (mh + 1) * HALF])
+        planes_first = at("planes_first", LOGS, [P, 4, QUARTER], BF16)
         for t in range(4):
-            scale_plane(1, t, 0, QUARTER, pick_first[:, t, :])
-        quantize_x(1, 0, QUARTER, NEG_LN_W + 3)
-        pick_second = at("pick_second", NEG_LN_W, [P, 4, QUARTER], F32)
-        pick_rest = at("pick_rest", NEG_LN_W + 4, [P, 4, HALF], F32)
+            scale_plane(1, t, planes_first, pick_first[:, t, :])
+        quantize_x(1, 0, QUARTER, NEG_LN_W, planes_first[:])
+        pick_second = at("pick_second", DAMP + 8, [P, 4, QUARTER], F32)
+        pick_rest = at("pick_rest", NEG_LN_W, [P, 4, HALF], F32)
         for picked, m0, width in ((pick_second, QUARTER, QUARTER), (pick_rest, HALF, HALF)):
             for t in range(4):
                 nc.vector.tensor_copy(
@@ -301,8 +301,8 @@ def tile_list_dryer_airflow_page_kernel(
             drift = at("drift%d" % mq, STAGE2 + 8 * (mq % 2) + 4, [P, 2, N], F32)
             for i in range(2):
                 cols = slice(mq * QUARTER + i * P, mq * QUARTER + (i + 1) * P)
-                phase = psum.tile([P, N], F32, name="phase", tag=BANKS[1])
-                line = psum.tile([P, N], F32, name="line", tag=BANKS[1])
+                phase = psum.tile([P, N], F32, name="phase", tag=BANKS[PRODUCT_BANKS[mq]])
+                line = psum.tile([P, N], F32, name="line", tag=BANKS[PRODUCT_BANKS[mq]])
                 for b in range(2):
                     nc.tensor.matmul_mx(
                         out=phase[:], lhsT=x_q[b][:, cols].bitcast(FP8X4), lhsT_scale=x_s[b][:, cols],
@@ -320,7 +320,7 @@ def tile_list_dryer_airflow_page_kernel(
             parts[mq] = (drift, wave)
 
         def place(mq, nb):
-            total = psum.tile([P, 2, P], F32, name="total", tag=BANKS[0])
+            total = psum.tile([P, 2, P], F32, name="total", tag=BANKS[1 - PRODUCT_BANKS[mq]])
             for k, part in enumerate(parts[mq]):
                 for i in range(2):
                     nc.tensor.matmul(
@@ -340,19 +340,23 @@ def tile_list_dryer_airflow_page_kernel(
                 nc.sync.dma_start(out=out[nb * P : (nb + 1) * P, :], in_=airflow[nb][:])
 
         products(0)
+        planes_second = at("planes_second", LOGS + 2, [P, 4, QUARTER], BF16)
         for t in range(4):
-            scale_plane(1, t, QUARTER, QUARTER, pick_second[:, t, :])
+            scale_plane(1, t, planes_second, pick_second[:, t, :])
         place(0, 0)
-        quantize_x(1, QUARTER, QUARTER, ROUNDED)
+        quantize_x(1, QUARTER, QUARTER, ROUNDED, planes_second[:])
+        for nb in range(1, 4):
+            place(0, nb)
+        planes_rest = at("planes_rest", STAGE2, [P, 4, HALF], BF16)
         for t in range(4):
-            scale_plane(1, t, HALF, HALF, pick_rest[:, t, :])
-        place(0, 1)
-        quantize_x(1, HALF, HALF, ROUNDED + 4)
-        place(0, 2)
-        place(0, 3)
+            scale_plane(1, t, planes_rest, pick_rest[:, t, :])
         products(1)
-        for nb in range(4):
-            place(1, nb)
+        place(1, 0)
+        quantize_x(1, 2 * QUARTER, QUARTER, ROUNDED + 2, planes_rest[:, :, 0:QUARTER])
+        place(1, 1)
+        quantize_x(1, 3 * QUARTER, QUARTER, ROUNDED + 4, planes_rest[:, :, QUARTER:HALF])
+        place(1, 2)
+        place(1, 3)
         products(2)
         place(2, 0)
         place(2, 1)

@@ -89,21 +89,16 @@ def tile_list_dryer_airflow_page_kernel(
         tab_sc = at("tab_sc", TAB_SCALES, [P, T], U8)
         nc.vector.memset(tab_sc[:].bitcast(I32), 0)
         w4_sc = at("w4_sc", W4 + 2, [P, 2, N], U8)
-        nc.gpsimd.memset(w4_sc[:].rearrange("p a c -> p (a c)").bitcast(I32), 0)
+        nc.vector.memset(w4_sc[:].rearrange("p a c -> p (a c)").bitcast(I32), 0)
 
         w1_raw = {}
         w1_raw[0, 0] = load_weight("w1_raw00", 0, w1[0:512, 0:HALF])
         idx = load_list("idx", offs)
-        idx2 = load_list("idx2", offs2)
-        idx3 = load_list("idx3", offs3)
-        idx4 = load_list("idx4", offs4)
-        gain_sb = at("gain_sb", SMALL + 0.5, [P, 2, 4], F32)
-        nc.sync.dma_start(out=gain_sb[:], in_=gain.rearrange("(b p t) -> p b t", b=2, t=4))
         wgs_sb = at("wgs_sb", WGS, [P, S], F32)
         nc.sync.dma_start(out=wgs_sb[:], in_=wgs)
         w1_raw[0, 1] = load_weight("w1_raw01", 1, w1[512:1024, 0:HALF])
         for q in range(4):
-            nc.sync.dma_start(
+            nc.gpsimd.dma_start(
                 out=tab_sc[32 * q : 32 * q + 12, :].bitcast(I32),
                 in_=tab_scales[:, 4 * q : 4 * q + 4, :].bitcast(I32),
             )
@@ -160,6 +155,7 @@ def tile_list_dryer_airflow_page_kernel(
         for a in range(3):
             w1_raw[1, a] = load_weight("w1_raw1%d" % a, (3 + a) % 4, w1[512 * a : 512 * (a + 1), HALF:H])
             prepare_w1(nc.vector.tensor_copy, 1, a)
+        idx2 = load_list("idx2", offs2)
         pages = {}
         gm_sb = {}
         gm_sb[0, 0] = at("gm00", GM, [P, 4, HALF], F32)
@@ -173,6 +169,9 @@ def tile_list_dryer_airflow_page_kernel(
             nc.sync.dma_start(out=gm_sb[b, jh][:], in_=dealt(gm, b)[:, :, jh * HALF : (jh + 1) * HALF])
 
         load_gm(0, 1)
+        idx3 = load_list("idx3", offs3)
+        gain_sb = at("gain_sb", SMALL + 0.5, [P, 2, 4], F32)
+        nc.sync.dma_start(out=gain_sb[:], in_=gain.rearrange("(b p t) -> p b t", b=2, t=4))
         for t in range(4):
             pages[1, t] = load_page("page1%d" % t, PAGE_HI + 8 * t, dealt(page0, 1)[:, t, :])
             if t == 0:
@@ -192,6 +191,8 @@ def tile_list_dryer_airflow_page_kernel(
         bias_sb = at("bias_sb", SMALL + 0.5625, [P, 4], F32)
         with nc.allow_non_contiguous_dma(reason="one bias value a partition"):
             nc.sync.dma_start(out=bias_sb[:], in_=bias.rearrange("(nb p) -> p nb", p=P))
+
+        idx4 = load_list("idx4", offs4)
 
         pick_lo = [at("pick_lo%d" % t, PICK_LO + 4 * t, [P, S], F32) for t in range(4)]
         pick_first = at("pick_first", WGS, [P, 4, QUARTER], F32)

from contextlib import ExitStack

import concourse.mybir as mybir
from concourse.masks import make_identity

K, T, S, H, T2, N = 1536, 4096, 1024, 1024, 2048, 512
FLOPS = 2 * K * H * S + 2 * 2 * H * N * S

F32 = mybir.dt.float32
BF16 = mybir.dt.bfloat16
I32 = mybir.dt.int32
U32 = mybir.dt.uint32
U16 = mybir.dt.uint16
U8 = mybir.dt.uint8
FP8X4 = mybir.dt.float8_e4m3fn_x4
FP4X4 = mybir.dt.float4_e2m1fn_x4
ACT = mybir.ActivationFunctionType
MULT = mybir.AluOpType.mult

P = 128
KB = 1024
HALF = 512
QUARTER = 256

TAB, PAGE_HI, PICK_LO, XQ = 0, 0, 32, 32
PAGE_LO, STAGE2, YS = 48, 48, 64
RAW = 80
GATHERED, TAB_SCALES, WGS = 112, 125, 129
ROUNDED = 133
W1Q, W2Q, W4 = 141, 156, 161
SMALL = 164
NEG_LN_W = 165
LOGS = 181
DAMP = 189
GM = 205
BANKS = ("even", "odd")
PRODUCT_BANKS = (1, 0, 1, 1)


def tile_list_dryer_airflow_page_kernel(
    tc, tab_words, tab_scales, offs, w1, gm, page0, wgs, offs2, offs3, gain,
    w2, w4_words, w4_scales, bias, page1, wgo, offs4, out,
):
    nc = tc.nc
    with ExitStack() as ctx:
        lists = ctx.enter_context(tc.tile_pool(name="lists", bufs=1))
        sbuf = ctx.enter_context(tc.tile_pool(name="sbuf", bufs=1))
        psum = ctx.enter_context(tc.psum_pool(name="psum", bufs=4))

        def at(name, kb, shape, dtype):
            return sbuf.tile(shape, dtype, name=name, offset=int(kb * KB), align_bytes=64)

        def load_list(name, src):
            tile = lists.tile([P, S // 16], U16, name=name)
            nc.sync.dma_start(tile[:], src)
            return tile

        def entries(tile, first, count):
            return tile[:, first // 16 : (first + count) // 16]

        def load_weight(name, slot, rows):
            raw = at(name, RAW + 8 * slot, [P, 4, HALF], F32)
            nc.sync.dma_start(out=raw[:], in_=rows.rearrange("(p j) c -> p j c", j=4))
            return raw

        def interleave(copy, name, kb, planes, width):
            woven = at(name, kb, [P, width, 4], BF16)
            copy(
                out=woven[:].rearrange("p (c i) j -> p c j i", i=4),
                in_=planes.rearrange("p j (c i) -> p c j i", i=4),
            )
            return woven

        def quantize(woven, codes, scales):
            nc.vector.quantize_mx(
                out=codes.bitcast(FP8X4), scales=scales, in_=woven[:].rearrange("p c j -> p (c j)")
            )

        def dealt(matrix, b):
            return matrix[b * HALF : (b + 1) * HALF, :].rearrange("(p t) c -> p t c", t=4)

        def load_page(name, kb, rows):
            tile = at(name, kb, [P, T2], F32)
            nc.sync.dma_start(out=tile[:], in_=rows)
            return tile

        ident = at("ident", SMALL, [P, P], F32)
        make_identity(nc, ident[:])
        tab_sc = at("tab_sc", TAB_SCALES, [P, T], U8)
        nc.vector.memset(tab_sc[:].bitcast(I32), 0)
        w4_sc = at("w4_sc", W4 + 2, [P, 2, N], U8)
        nc.vector.memset(w4_sc[:].rearrange("p a c -> p (a c)").bitcast(I32), 0)

        w1_raw = {}
        w1_raw[0, 0] = load_weight("w1_raw00", 0, w1[0:512, 0:HALF])
        idx = load_list("idx", offs)
        wgs_sb = at("wgs_sb", WGS, [P, S], F32)
        nc.sync.dma_start(out=wgs_sb[:], in_=wgs)
        w1_raw[0, 1] = load_weight("w1_raw01", 1, w1[512:1024, 0:HALF])
        for q in range(4):
            nc.gpsimd.dma_start(
                out=tab_sc[32 * q : 32 * q + 12, :].bitcast(I32),
                in_=tab_scales[:, 4 * q : 4 * q + 4, :].bitcast(I32),
            )
        w1_raw[0, 2] = load_weight("w1_raw02", 2, w1[1024:1536, 0:HALF])
        tab = []
        for a in range(3):
            words = at("tab%d" % a, TAB + 16 * a, [P, T], I32)
            nc.sync.dma_start(out=words[:], in_=tab_words[a].rearrange("p n t -> p (n t)").bitcast(I32))
            tab.append(words)

        w1_q = {}
        w1_s = {}

        def prepare_w1(copy, b, a):
            n = 3 * b + a
            woven = interleave(copy, "w1_bf%d" % n, ROUNDED + 4 * (n % 2), w1_raw[b, a][:], HALF)
            w1_q[b, a] = at("w1_q%d" % n, W1Q + 2 * n, [P, HALF], U32)
            w1_s[b, a] = at("w1_s%d" % n, W1Q + 12 + n / 2, [P, HALF], U8)
            quantize(woven, w1_q[b, a][:], w1_s[b, a][:])

        for a in range(3):
            prepare_w1(nc.vector.tensor_copy, 0, a)

        ln_w = at("ln_w", DAMP + 8, [P, 32, 32], F32)
        for half in range(2):
            bank = psum.tile([P, 4, P], F32, name="bank", tag=BANKS[1])
            for i in range(4):
                jb = 4 * half + i
                nc.tensor.transpose(bank[:, i, :], wgs_sb[:, jb * P : (jb + 1) * P], ident[:])
            nc.scalar.activation(
                out=ln_w[:, 16 * half : 16 * half + 16, :].rearrange("p (i t) m -> p i t m", t=4),
                in_=bank[:].rearrange("p i (m t) -> p i t m", t=4),
                func=ACT.Ln,
            )
        neg_ln_w = at("neg_ln_w", NEG_LN_W, [P, 32, P], F32)
        for q in range(4):
            nc.scalar.activation(
                out=neg_ln_w[:, :, 32 * q : 32 * q + 32], in_=ln_w[:], func=ACT.Copy, scale=-1.0
            )

        v_s = at("v_s", GATHERED + 12, [P, S], U8)
        nc.vector.tensor_copy(v_s[:], tab_sc[:].indirect(idx[:]))
        v_q = []
        for a in range(3):
            picked = at("v_q%d" % a, GATHERED + 4 * a, [P, S], U32)
            width = HALF if a == 2 else S
            for j0 in range(0, S, width):
                nc.vector.tensor_copy(
                    picked[:, j0 : j0 + width],
                    tab[a][:].bitcast(U32).indirect(entries(idx, j0, width)),
                )
            v_q.append(picked)

        for a in range(3):
            w1_raw[1, a] = load_weight("w1_raw1%d" % a, (3 + a) % 4, w1[512 * a : 512 * (a + 1), HALF:H])
            prepare_w1(nc.vector.tensor_copy, 1, a)
        idx2 = load_list("idx2", offs2)
        pages = {}
        gm_sb = {}
        gm_sb[0, 0] = at("gm00", GM, [P, 4, HALF], F32)
        for t in range(4):
            pages[0, t] = load_page("page0%d" % t, PAGE_LO + 8 * t, dealt(page0, 0)[:, t, :])
            nc.sync.dma_start(out=gm_sb[0, 0][:, t, :], in_=dealt(gm, 0)[:, t, 0:HALF])

        def load_gm(b, jh):
            n = 2 * b + jh
            gm_sb[b, jh] = at("gm%d%d" % (b, jh), GM + 8 * (n % 3), [P, 4, HALF], F32)
            nc.sync.dma_start(out=gm_sb[b, jh][:], in_=dealt(gm, b)[:, :, jh * HALF : (jh + 1) * HALF])

        load_gm(0, 1)
        idx3 = load_list("idx3", offs3)
        gain_sb = at("gain_sb", SMALL + 0.5, [P, 2, 4], F32)
        nc.sync.dma_start(out=gain_sb[:], in_=gain.rearrange("(b p t) -> p b t", b=2, t=4))
        for t in range(4):
            pages[1, t] = load_page("page1%d" % t, PAGE_HI + 8 * t, dealt(page0, 1)[:, t, :])
            if t == 0:
                load_gm(1, 0)
        w2_raw = [load_weight("w2_raw%d" % b, 2 + b, w2[b * HALF : (b + 1) * HALF, :]) for b in range(2)]
        w4_q = at("w4_q", W4, [P, 2, 2 * N], U8)
        nc.sync.dma_start(
            out=w4_q[:].bitcast(I32), in_=w4_words.rearrange("a p c -> p a c").bitcast(I32)
        )
        for q in range(4):
            nc.sync.dma_start(
                out=w4_sc[32 * q : 32 * q + 4, :, :].bitcast(I32),
                in_=w4_scales[:, 4 * q : 4 * q + 4, :].rearrange("a r c -> r a c").bitcast(I32),
            )
        wgo_sb = at("wgo_sb", TAB_SCALES, [P, S], F32)
        nc.sync.dma_start(out=wgo_sb[:], in_=wgo)
        bias_sb = at("bias_sb", SMALL + 0.5625, [P, 4], F32)
        with nc.allow_non_contiguous_dma(reason="one bias value a partition"):
            nc.sync.dma_start(out=bias_sb[:], in_=bias.rearrange("(nb p) -> p nb", p=P))

        idx4 = load_list("idx4", offs4)

        pick_lo = [at("pick_lo%d" % t, PICK_LO + 4 * t, [P, S], F32) for t in range(4)]
        pick_first = at("pick_first", WGS, [P, 4, QUARTER], F32)
        damp = {}

        def stage_one(b, jh):
            logs = at("logs%d%d" % (b, jh), LOGS, [P, 4, HALF], F32)
            for i in range(4):
                cols = slice(jh * HALF + i * P, jh * HALF + (i + 1) * P)
                hum = psum.tile([P, HALF], F32, name="hum", tag=BANKS[jh])
                for a in range(3):
                    nc.tensor.matmul_mx(
                        out=hum[:],
                        lhsT=v_q[a][:, cols].bitcast(FP8X4),
                        lhsT_scale=v_s[4 * a : P, cols],
                        rhs=w1_q[b, a][:].bitcast(FP8X4),
                        rhs_scale=w1_s[b, a][:],
                        start=(a == 0),
                        stop=(a == 2),
                    )
                nc.scalar.activation(
                    out=logs[:, i, :].rearrange("p (t m) -> p t m", t=4),
                    in_=hum[:].rearrange("p (m t) -> p t m", t=4),
                    func=ACT.Abs,
                )
                nc.scalar.activation(out=logs[:, i, :], in_=logs[:, i, :], func=ACT.Ln, bias=1.0)
            damp[b, jh] = at("damp%d%d" % (b, jh), DAMP + 8 * jh, [P, 4, HALF], F32)
            for t in range(4):
                total = psum.tile([P, 4, P], F32, name="total", tag=BANKS[1 - jh])
                for i in range(4):
                    nc.tensor.matmul(
                        total[:, i, :], lhsT=neg_ln_w[:, 16 * jh + 4 * i + t, :], rhs=ident[:],
                        is_transpose=True, start=(i == 0), stop=False,
                    )
                for i in range(4):
                    nc.tensor.matmul(
                        total[:, i, :], lhsT=logs[:, i, t * P : (t + 1) * P], rhs=ident[:],
                        is_transpose=True, start=False, stop=(i == 3),
                    )
                nc.scalar.activation(
                    out=damp[b, jh][:, t, :], in_=total[:].rearrange("p i j -> p (i j)"),
                    func=ACT.Exp, scale=-1.0,
                )
                nc.vector.tensor_tensor(
                    pages[b, t][:].indirect(entries(idx2, jh * HALF, HALF)),
                    damp[b, jh][:, t, :], gm_sb[b, jh][:, t, :], MULT,
                )
                if jh == 1 and b == 0:
                    nc.vector.tensor_copy(pick_lo[t][:], pages[b, t][:].indirect(idx3[:]))
                if jh == 1 and b == 1:
                    nc.vector.tensor_copy(
                        pick_first[:, t, :], pages[b, t][:].indirect(entries(idx3, 0, QUARTER))
                    )

        stage_one(0, 0)
        load_gm(1, 1)
        stage_one(0, 1)
        airflow = [load_page("air%d" % nb, RAW + 8 * nb, page1[nb * P : (nb + 1) * P, :]) for nb in range(2)]
        stage_one(1, 0)
        stage_one(1, 1)

        table_warm = at("table_warm", SMALL + 0.625, [P, 1], F32)
        nc.scalar.activation(out=table_warm[:], in_=damp[1, 1][:, 3, 0:1], func=ACT.Sin, scale=0.0)

        w2_q = at("w2_q", W2Q, [P, 2, N], U32)
        w2_s = at("w2_s", W2Q + 4, [P, 2, N], U8)
        for b in range(2):
            woven = interleave(nc.scalar.copy, "w2_bf%d" % b, ROUNDED + 4 * b, w2_raw[b][:], N)
            quantize(woven, w2_q[:, b, :], w2_s[:, b, :])
        for nb in range(2, 4):
            airflow.append(load_page("air%d" % nb, RAW + 8 * nb, page1[nb * P : (nb + 1) * P, :]))

        def scale_plane(b, t, planes, picked):
            nc.scalar.activation(
                out=planes[:, t, :], in_=picked, func=ACT.Copy, scale=gain_sb[:, b, t : t + 1]
            )

        planes_lo = at("planes_lo", LOGS, [P, 4, S], BF16)
        for t in range(4):
            scale_plane(0, t, planes_lo, pick_lo[t][:])
        x_q = [at("x_q%d" % b, XQ + 4 * b, [P, S], U32) for b in range(2)]
        x_s = [at("x_s%d" % b, XQ + 8 + b, [P, S], U8) for b in range(2)]

        def quantize_x(b, m0, width, kb, planes):
            cols = slice(m0, m0 + width)
            woven = interleave(nc.scalar.copy, "x_bf%d_%d" % (b, m0), kb, planes, width)
            quantize(woven, x_q[b][:, cols], x_s[b][:, cols])

        for mh in range(2):
            quantize_x(0, mh * HALF, HALF, GM + 8 + 4 * mh, planes_lo[:, :, mh * HALF : (mh + 1) * HALF])
        planes_first = at("planes_first", LOGS, [P, 4, QUARTER], BF16)
        for t in range(4):
            scale_plane(1, t, planes_first, pick_first[:, t, :])
        quantize_x(1, 0, QUARTER, NEG_LN_W, planes_first[:])
        pick_second = at("pick_second", DAMP + 8, [P, 4, QUARTER], F32)
        pick_rest = at("pick_rest", NEG_LN_W, [P, 4, HALF], F32)
        for picked, m0, width in ((pick_second, QUARTER, QUARTER), (pick_rest, HALF, HALF)):
            for t in range(4):
                nc.vector.tensor_copy(
                    picked[:, t, :], pages[1, t][:].indirect(entries(idx3, m0, width))
                )

        parts = {}

        def products(mq):
            wave = at("wave%d" % mq, STAGE2 + 8 * (mq % 2), [P, 2, N], F32)
            drift = at("drift%d" % mq, STAGE2 + 8 * (mq % 2) + 4, [P, 2, N], F32)
            for i in range(2):
                cols = slice(mq * QUARTER + i * P, mq * QUARTER + (i + 1) * P)
                phase = psum.tile([P, N], F32, name="phase", tag=BANKS[PRODUCT_BANKS[mq]])
                line = psum.tile([P, N], F32, name="line", tag=BANKS[PRODUCT_BANKS[mq]])
                for b in range(2):
                    nc.tensor.matmul_mx(
                        out=phase[:], lhsT=x_q[b][:, cols].bitcast(FP8X4), lhsT_scale=x_s[b][:, cols],
                        rhs=w2_q[:, b, :].bitcast(FP8X4), rhs_scale=w2_s[:, b, :],
                        start=(b == 0), stop=(b == 1),
                    )
                for b in range(2):
                    nc.tensor.matmul_mx(
                        out=line[:], lhsT=x_q[b][:, cols].bitcast(FP8X4), lhsT_scale=x_s[b][:, cols],
                        rhs=w4_q[:, b, :].bitcast(FP4X4), rhs_scale=w4_sc[:, b, :],
                        start=(b == 0), stop=(b == 1),
                    )
                nc.scalar.activation(out=wave[:, i, :], in_=phase[:], func=ACT.Sin)
                nc.scalar.copy(out=drift[:, i, :], in_=line[:])
            parts[mq] = (drift, wave)

        def place(mq, nb):
            total = psum.tile([P, 2, P], F32, name="total", tag=BANKS[1 - PRODUCT_BANKS[mq]])
            for k, part in enumerate(parts[mq]):
                for i in range(2):
                    nc.tensor.matmul(
                        total[:, i, :], lhsT=part[:, i, nb * P : (nb + 1) * P], rhs=ident[:],
                        is_transpose=True, start=(k == 0 and i == 0), stop=(k == 1 and i == 1),
                    )
            y = at("y%d%d" % (mq, nb), YS + 4 * mq + nb, [P, QUARTER], F32)
            nc.scalar.activation(
                out=y[:], in_=total[:].rearrange("p i m -> p (i m)"), func=ACT.Identity,
                bias=bias_sb[:, nb : nb + 1],
            )
            nc.vector.tensor_tensor(
                airflow[nb][:].indirect(entries(idx4, mq * QUARTER, QUARTER)),
                y[:], wgo_sb[:, mq * QUARTER : (mq + 1) * QUARTER], MULT,
            )
            if mq == 3:
                nc.sync.dma_start(out=out[nb * P : (nb + 1) * P, :], in_=airflow[nb][:])

        products(0)
        planes_second = at("planes_second", LOGS + 2, [P, 4, QUARTER], BF16)
        for t in range(4):
            scale_plane(1, t, planes_second, pick_second[:, t, :])
        place(0, 0)
        quantize_x(1, QUARTER, QUARTER, ROUNDED, planes_second[:])
        for nb in range(1, 4):
            place(0, nb)
        planes_rest = at("planes_rest", STAGE2, [P, 4, HALF], BF16)
        for t in range(4):
            scale_plane(1, t, planes_rest, pick_rest[:, t, :])
        products(1)
        place(1, 0)
        quantize_x(1, 2 * QUARTER, QUARTER, ROUNDED + 2, planes_rest[:, :, 0:QUARTER])
        place(1, 1)
        quantize_x(1, 3 * QUARTER, QUARTER, ROUNDED + 4, planes_rest[:, :, QUARTER:HALF])
        place(1, 2)
        place(1, 3)
        products(2)
        place(2, 0)
        place(2, 1)
        products(3)
        for nb in range(4):
            place(3, nb)
            if nb < 2:
                place(2, nb + 2)
